import numpy as np
import ml_dtypes


def mxq(x, axis, fmt="e4m3"):
    dtype, down = {"e4m3": (ml_dtypes.float8_e4m3fn, 7), "e5m2": (ml_dtypes.float8_e5m2, 14)}[fmt]
    v = np.moveaxis(np.asarray(x, np.float32).astype(ml_dtypes.bfloat16).astype(np.float64), axis, -1)
    blocks = v.reshape(v.shape[:-1] + (-1, 32))
    amax = np.abs(blocks).max(-1, keepdims=True)
    byte = np.maximum(np.where(amax > 0, np.frexp(amax)[1] - 1 + 127, 0) - down, 1)
    scale = np.exp2(byte - 127.0)
    codes = (blocks / scale).astype(np.float32).astype(dtype).astype(np.float64)
    return np.moveaxis((codes * scale).reshape(v.shape), -1, axis)


WIDE = False


def mx_kscale(k, group=512):
    if not WIDE:
        return np.ones(k)
    levels = np.array([10, -10, 5, -5, 0])
    if group != 512:
        return np.exp2(np.random.permutation(np.resize(levels, k // group))).repeat(group)
    if k % 512:
        return np.exp2(np.random.permutation(np.resize(levels, k // 32))).repeat(32)
    a = np.empty((k // 512, 16))
    for p in range(k // 512):
        a[p, :8] = np.random.permutation(np.resize(levels, 8))
        for g in range(8):
            far = levels[np.abs(levels - a[p, g]) >= 10]
            a[p, g + 8] = far[np.random.randint(len(far))]
    return np.exp2(a.ravel()).repeat(32)


def f64(x):
    return np.asarray(x).astype(np.float64)


def striped(idx):
    return np.tile(np.asarray(idx).reshape(-1, 16).T, (8, 1)).astype(np.uint16)


def unstriped(offs):
    return offs[:16].T.reshape(-1).astype(np.int64)


H, KV, D, NQ, N = 4, 4, 128, 512, 1024
CAP = 2.0


def setup_inputs():
    n = np.random.standard_normal
    s = mx_kscale(D, 0)[:, None]
    u = mx_kscale(N)
    t = np.random.uniform(0.5, 2.0, N) * u
    v = n((KV, N, 128))
    v[:, :, 127] = 1.0
    return {
        "qT": (n((H, D, NQ)) * s * (0.70 / np.sqrt(D))).astype(np.float32),
        "kT": (n((KV, D, N)) / s).astype(np.float32),
        "t": t.reshape(N, 1).astype(np.float32),
        "v": (v / t[:, None]).astype(np.float32),
    }


def reference(qT, kT, t, v):
    a = mxq(f64(kT), 1, "e4m3").transpose(0, 2, 1) @ mxq(f64(qT), 1, "e4m3")
    a = CAP * np.tanh(a / CAP)
    p = np.exp(a)
    w = p * f64(t)
    y = mxq(w, 1, "e4m3").transpose(0, 2, 1) @ mxq(f64(v), 1, "e4m3")
    y = y / (y[:, :, 127:128])
    return y

@@ -1,0 +1,215 @@
+from contextlib import ExitStack
+
+import concourse.mybir as mybir
+
+H, D, NQ, N = 4, 128, 512, 1024
+CAP = 2.0
+FLOPS = 2 * 2 * H * NQ * N * D
+
+F32 = mybir.dt.float32
+BF16 = mybir.dt.bfloat16
+U32 = mybir.dt.uint32
+U8 = mybir.dt.uint8
+FP8X4 = mybir.dt.float8_e4m3fn_x4
+ACT = mybir.ActivationFunctionType
+ALU = mybir.AluOpType
+
+P = 128
+PACK = 4
+ROWS = D // PACK
+K_PASS = P * PACK
+TILE = 128
+CHUNKS = NQ // TILE
+PASSES = N // K_PASS
+
+GROUPS = [(0, 0), (0, 1), (1, 0), (1, 1), (0, 2), (1, 2), (0, 3), (1, 3)]
+UNITS = [(g, c, h) for g, c in GROUPS for h in range(H)]
+LAST_GROUP = len(UNITS) - H
+SPANS = [(u, u + 1) for u in range(0, LAST_GROUP, 2)] + [(u,) for u in range(LAST_GROUP, len(UNITS))]
+
+
+def tile_rows_cap_kernel(tc, qT, kT, t, v, out):
+    nc = tc.nc
+    q_rows = qT.rearrange("h d q -> (h d) q").rearrange("(p j) q -> p j q", j=PACK)
+    k_rows = kT.rearrange("h d n -> (h d) n").rearrange("(p j) n -> p j n", j=PACK)
+
+    with ExitStack() as ctx:
+        keep = ctx.enter_context(tc.tile_pool(name="keep", bufs=1))
+        work = ctx.enter_context(tc.tile_pool(name="work", bufs=1))
+        score_pool = ctx.enter_context(tc.psum_pool(name="scores", bufs=1))
+        y_pool = ctx.enter_context(tc.psum_pool(name="y", bufs=4))
+        ctx.enter_context(tc.manual_schedule())
+
+        def load(name, src):
+            raw = keep.tile([P] + list(src.shape[1:]), F32, name=name, align_bytes=64)
+            nc.sync.dma_start(out=raw[:], in_=src)
+            return raw
+
+        def mx_tiles(name, words):
+            codes = keep.tile([P, words], U32, name=name + "_codes", align_bytes=64)
+            scales = keep.tile([P, words], U8, name=name + "_scales", align_bytes=64)
+            return codes, scales
+
+        def quantize(mx, first, last, packed):
+            codes, scales = mx
+            nc.vector.quantize_mx(out=codes[:, first:last].bitcast(FP8X4), scales=scales[:, first:last],
+                                  in_=packed[:, PACK * first:PACK * last])
+
+        half = K_PASS // 2
+        q_first = load("q_first", q_rows[:, :, 0:TILE])
+        k0_halves = [load("k0_%d" % i, k_rows[:, :, i * half:(i + 1) * half]) for i in range(2)]
+        t_tile = keep.tile([P, PASSES, 8], F32, name="t_tile", align_bytes=64)
+        nc.sync.dma_start(out=t_tile[:, :, 0:PACK], in_=t.rearrange("(g p j) o -> p g (j o)", g=PASSES, j=PACK))
+        q_rest = load("q_rest", q_rows[:, :, TILE:NQ])
+        k1_raw = load("k1", k_rows[:, :, K_PASS:N])
+        v_raw = [load("v%d" % g, v[:, g * K_PASS:(g + 1) * K_PASS, :].rearrange("h (p j) e -> p h (j e)", j=PACK))
+                 for g in range(PASSES)]
+
+        q_bf = keep.tile([P, NQ * PACK], BF16, name="q_bf", align_bytes=64)
+        k_bf = [keep.tile([P, K_PASS * PACK], BF16, name="k_bf%d" % g, align_bytes=64) for g in range(PASSES)]
+        v_bf = [keep.tile([P, H * D * PACK], BF16, name="v_bf%d" % g, align_bytes=64) for g in range(PASSES)]
+        q_mx = mx_tiles("q", NQ)
+        k_mx = [mx_tiles("k%d" % g, K_PASS) for g in range(PASSES)]
+        v_mx = [mx_tiles("v%d" % g, H * D) for g in range(PASSES)]
+
+        def pack_q(raw, first, last):
+            dst = q_bf[:, PACK * first:PACK * last].rearrange("p (c i j) -> p c j i", i=4, j=PACK)
+            nc.vector.tensor_copy(out=dst, in_=raw[:].rearrange("p j (c i) -> p c j i", i=4))
+
+        def pack_k(raw, g, first, last):
+            dst = k_bf[g][:].rearrange("p (r s j) -> p s j r", r=PACK, j=PACK)[:, first:last]
+            nc.vector.tensor_copy(out=dst, in_=raw[:].rearrange("p j (s r) -> p s j r", r=PACK))
+
+        def pack_v(g):
+            dst = v_bf[g][:].rearrange("p (h c i j) -> p h c j i", h=H, i=4, j=PACK)
+            nc.vector.tensor_copy(out=dst, in_=v_raw[g][:].rearrange("p h (j c i) -> p h c j i", j=PACK, i=4))
+
+        score_banks = [score_pool.tile([P, PACK * TILE], F32, name="scores%d" % h) for h in range(H)]
+
+        def scores(u):
+            g, c, h = UNITS[u]
+            rows = slice(ROWS * h, ROWS * (h + 1))
+            cols = slice(TILE * c, TILE * (c + 1))
+            for r in range(PACK):
+                place = slice(TILE * r, TILE * (r + 1))
+                nc.tensor.matmul_mx(out=score_banks[h][:, place],
+                                    lhsT=k_mx[g][0][rows, place].bitcast(FP8X4), lhsT_scale=k_mx[g][1][rows, place],
+                                    rhs=q_mx[0][rows, cols].bitcast(FP8X4), rhs_scale=q_mx[1][rows, cols],
+                                    start=True, stop=True)
+
+        capped, probs, weights, w_mx, y_tiles, recips = {}, {}, {}, {}, {}, {}
+        span_of = {u: (n, i) for n, span in enumerate(SPANS) for i, u in enumerate(span)}
+
+        def cap(u):
+            n, i = span_of[u]
+            if i == 0:
+                capped[n] = work.tile([P, len(SPANS[n]) * K_PASS], F32, name="capped", bufs=4, align_bytes=64)
+            dst = capped[n][:, i * K_PASS:(i + 1) * K_PASS].rearrange("p (q r) -> p q r", r=PACK)
+            src = score_banks[UNITS[u][2]][:].rearrange("p (r q) -> p q r", r=PACK)
+            nc.scalar.activation(out=dst, in_=src, func=ACT.Tanh, scale=1.0 / CAP)
+            if u + H < len(UNITS):
+                scores(u + H)
+
+        def exponentiate(n):
+            probs[n] = work.tile([P, len(SPANS[n]) * K_PASS], F32, name="probs", bufs=8, align_bytes=64)
+            nc.scalar.activation(out=probs[n][:], in_=capped[n][:], func=ACT.Exp, scale=CAP)
+
+        def weigh(n):
+            cols = len(SPANS[n]) * TILE
+            g = UNITS[SPANS[n][0]][0]
+            weights[n] = work.tile([P, cols * PACK], BF16, name="weights", bufs=4, align_bytes=64)
+            nc.vector.tensor_tensor(out=weights[n][:].rearrange("p (q r) -> p q r", r=PACK),
+                                    in0=probs[n][:].rearrange("p (q r) -> p q r", r=PACK),
+                                    in1=t_tile[:, g, 0:PACK].unsqueeze(1).to_broadcast([P, cols, PACK]),
+                                    op=ALU.mult)
+
+        def quantize_weights(n):
+            cols = len(SPANS[n]) * TILE
+            w_mx[n] = mx_tiles("w%d" % n, cols)
+            quantize(w_mx[n], 0, cols, weights[n])
+
+        def y_slot(c, h):
+            key = (c, h) if c == CHUNKS - 1 else (c, 0)
+            heads = 1 if c == CHUNKS - 1 else H
+            if key not in y_tiles:
+                y_tiles[key] = y_pool.tile([P, heads, D], F32, name="y")
+            return y_tiles[key][:, h - key[1], :]
+
+        def value_pass(g, c, h):
+            n, i = span_of[UNITS.index((g, c, h))]
+            place = slice(TILE * i, TILE * (i + 1))
+            cols = slice(D * h, D * (h + 1))
+            nc.tensor.matmul_mx(out=y_slot(c, h),
+                                lhsT=w_mx[n][0][:, place].bitcast(FP8X4), lhsT_scale=w_mx[n][1][:, place],
+                                rhs=v_mx[g][0][:, cols].bitcast(FP8X4), rhs_scale=v_mx[g][1][:, cols],
+                                start=(g == 0), stop=(g == PASSES - 1))
+
+        def values(n):
+            done = None
+            for u in SPANS[n]:
+                g, c, h = UNITS[u]
+                if c == CHUNKS - 1:
+                    value_pass(g, c, h)
+                    if g == PASSES - 1:
+                        done = (c, h)
+                elif g == PASSES - 1:
+                    for each in range(PASSES):
+                        value_pass(each, c, h)
+                    if h == H - 1:
+                        done = (c, 0)
+            return done
+
+        def invert(key):
+            y = y_tiles[key]
+            heads = y.shape[1]
+            recips[key] = work.tile([P, heads, 1], F32, name="recip", bufs=4, align_bytes=64)
+            nc.vector.reciprocal(out=recips[key][:], in_=y[:, :, D - 1:D])
+
+        def normalize(key):
+            c, h0 = key
+            y = y_tiles[key]
+            heads = y.shape[1]
+            res = work.tile([P, heads, D], F32, name="res", bufs=4, align_bytes=64)
+            nc.vector.tensor_tensor(out=res[:], in0=y[:], in1=recips[key][:].to_broadcast([P, heads, D]), op=ALU.mult)
+            dst = out[h0:h0 + heads, TILE * c:TILE * (c + 1), :].rearrange("h q e -> q h e")
+            nc.sync.dma_start(out=dst, in_=res[:])
+
+        pack_q(q_first, 0, TILE)
+        pack_k(k0_halves[0], 0, 0, P // 2)
+        quantize(q_mx, 0, TILE, q_bf)
+        pack_k(k0_halves[1], 0, P // 2, P)
+        for r in range(PACK):
+            quantize(k_mx[0], TILE * r, TILE * (r + 1), k_bf[0])
+        for u in range(H):
+            scores(u)
+        pack_q(q_rest, TILE, NQ)
+        quantize(q_mx, TILE, 2 * TILE, q_bf)
+        quantize(q_mx, 2 * TILE, NQ, q_bf)
+        pack_k(k1_raw, 1, 0, P)
+
+        extras = [
+            lambda: quantize(k_mx[1], 0, K_PASS, k_bf[1]),
+            lambda: pack_v(0),
+            lambda: quantize(v_mx[0], 0, H * D, v_bf[0]),
+            lambda: pack_v(1),
+            lambda: quantize(v_mx[1], 0, H * D, v_bf[1]),
+        ]
+        cap(0)
+        next_unit = 1
+        for n, span in enumerate(SPANS):
+            while next_unit <= min(span[-1] + 1, len(UNITS) - 1):
+                cap(next_unit)
+                next_unit = next_unit + 1
+            exponentiate(n)
+            done = values(n - 1) if n > 0 else None
+            weigh(n)
+            if n < len(extras):
+                extras[n]()
+            if done is not None:
+                invert(done)
+            quantize_weights(n)
+            if done is not None:
+                normalize(done)
+        done = values(len(SPANS) - 1)
+        invert(done)
+        normalize(done)

@@ -22,6 +22,7 @@ TILE = 128
 CHUNKS = NQ // TILE
 PASSES = N // K_PASS
 
+SCALAR_SHARE = 20
 GROUPS = [(0, 0), (0, 1), (1, 0), (1, 1), (0, 2), (1, 2), (0, 3), (1, 3)]
 UNITS = [(g, c, h) for g, c in GROUPS for h in range(H)]
 LAST_GROUP = len(UNITS) - H
@@ -76,9 +77,10 @@ def tile_rows_cap_kernel(tc, qT, kT, t, v, out):
             dst = q_bf[:, PACK * first:PACK * last].rearrange("p (c i j) -> p c j i", i=4, j=PACK)
             nc.vector.tensor_copy(out=dst, in_=raw[:].rearrange("p j (c i) -> p c j i", i=4))
 
-        def pack_k(raw, g, first, last):
-            dst = k_bf[g][:].rearrange("p (r s j) -> p s j r", r=PACK, j=PACK)[:, first:last]
-            nc.vector.tensor_copy(out=dst, in_=raw[:].rearrange("p j (s r) -> p s j r", r=PACK))
+        def pack_k(copy, raw, raw_first, g, first, last):
+            dst = k_bf[g][:].rearrange("p (r s j) -> p s r j", r=PACK, j=PACK)[:, first:last]
+            src = raw[:].rearrange("p j (s r) -> p s r j", r=PACK)[:, first - raw_first:last - raw_first]
+            copy(out=dst, in_=src)
 
         def pack_v(g):
             dst = v_bf[g][:].rearrange("p (h c i j) -> p h c j i", h=H, i=4, j=PACK)
@@ -100,33 +102,36 @@ def tile_rows_cap_kernel(tc, qT, kT, t, v, out):
         capped, probs, weights, w_mx, y_tiles, recips = {}, {}, {}, {}, {}, {}
         span_of = {u: (n, i) for n, span in enumerate(SPANS) for i, u in enumerate(span)}
 
-        def cap(u):
+        def span_tile(table, n, name, dtype, bufs):
+            if n not in table:
+                table[n] = work.tile([P, len(SPANS[n]) * K_PASS], dtype, name=name, bufs=bufs, align_bytes=64)
+            return table[n]
+
+        def words(tile, first, last):
+            return tile[:, PACK * first:PACK * last].rearrange("p (q r) -> p q r", r=PACK)
+
+        def cap(u, first=0, last=TILE):
             n, i = span_of[u]
-            if i == 0:
-                capped[n] = work.tile([P, len(SPANS[n]) * K_PASS], F32, name="capped", bufs=4, align_bytes=64)
-            dst = capped[n][:, i * K_PASS:(i + 1) * K_PASS].rearrange("p (q r) -> p q r", r=PACK)
-            src = score_banks[UNITS[u][2]][:].rearrange("p (r q) -> p q r", r=PACK)
+            dst = words(span_tile(capped, n, "capped", F32, 4), i * TILE + first, i * TILE + last)
+            src = score_banks[UNITS[u][2]][:].rearrange("p (r q) -> p q r", r=PACK)[:, first:last]
             nc.scalar.activation(out=dst, in_=src, func=ACT.Tanh, scale=1.0 / CAP)
-            if u + H < len(UNITS):
-                scores(u + H)
 
-        def exponentiate(n):
-            probs[n] = work.tile([P, len(SPANS[n]) * K_PASS], F32, name="probs", bufs=8, align_bytes=64)
-            nc.scalar.activation(out=probs[n][:], in_=capped[n][:], func=ACT.Exp, scale=CAP)
+        def exponentiate(n, first, last):
+            cols = slice(PACK * first, PACK * last)
+            nc.scalar.activation(out=span_tile(probs, n, "probs", F32, 8)[:, cols], in_=capped[n][:, cols],
+                                 func=ACT.Exp, scale=CAP)
 
-        def weigh(n):
-            cols = len(SPANS[n]) * TILE
+        def weigh(n, first, last):
             g = UNITS[SPANS[n][0]][0]
-            weights[n] = work.tile([P, cols * PACK], BF16, name="weights", bufs=4, align_bytes=64)
-            nc.vector.tensor_tensor(out=weights[n][:].rearrange("p (q r) -> p q r", r=PACK),
-                                    in0=probs[n][:].rearrange("p (q r) -> p q r", r=PACK),
-                                    in1=t_tile[:, g, 0:PACK].unsqueeze(1).to_broadcast([P, cols, PACK]),
+            nc.vector.tensor_tensor(out=words(span_tile(weights, n, "weights", BF16, 4), first, last),
+                                    in0=words(probs[n], first, last),
+                                    in1=t_tile[:, g, 0:PACK].unsqueeze(1).to_broadcast([P, last - first, PACK]),
                                     op=ALU.mult)
 
-        def quantize_weights(n):
-            cols = len(SPANS[n]) * TILE
-            w_mx[n] = mx_tiles("w%d" % n, cols)
-            quantize(w_mx[n], 0, cols, weights[n])
+        def quantize_weights(n, first, last):
+            if n not in w_mx:
+                w_mx[n] = mx_tiles("w%d" % n, len(SPANS[n]) * TILE)
+            quantize(w_mx[n], first, last, weights[n])
 
         def y_slot(c, h):
             key = (c, h) if c == CHUNKS - 1 else (c, 0)
@@ -171,21 +176,35 @@ def tile_rows_cap_kernel(tc, qT, kT, t, v, out):
             heads = y.shape[1]
             res = work.tile([P, heads, D], F32, name="res", bufs=4, align_bytes=64)
             nc.vector.tensor_tensor(out=res[:], in0=y[:], in1=recips[key][:].to_broadcast([P, heads, D]), op=ALU.mult)
+            store(key, res)
+
+        def normalize_on_scalar(key):
+            res = work.tile([P, 1, D], F32, name="res", bufs=4, align_bytes=64)
+            nc.scalar.activation(out=res[:, 0, :], in_=y_tiles[key][:, 0, :], func=ACT.Copy, scale=recips[key][:, 0, :])
+            store(key, res)
+
+        def store(key, res):
+            c, h0 = key
+            heads = res.shape[1]
             dst = out[h0:h0 + heads, TILE * c:TILE * (c + 1), :].rearrange("h q e -> q h e")
             nc.sync.dma_start(out=dst, in_=res[:])
 
         pack_q(q_first, 0, TILE)
-        pack_k(k0_halves[0], 0, 0, P // 2)
+        mid = P // 2
+        pack_k(nc.vector.tensor_copy, k0_halves[0], 0, 0, 0, mid)
         quantize(q_mx, 0, TILE, q_bf)
-        pack_k(k0_halves[1], 0, P // 2, P)
         for r in range(PACK):
-            quantize(k_mx[0], TILE * r, TILE * (r + 1), k_bf[0])
+            quantize(k_mx[0], TILE * r, TILE * r + mid, k_bf[0])
+        pack_k(nc.vector.tensor_copy, k0_halves[1], mid, 0, mid, P - SCALAR_SHARE)
+        pack_k(nc.scalar.copy, k0_halves[1], mid, 0, P - SCALAR_SHARE, P)
+        for r in range(PACK):
+            quantize(k_mx[0], TILE * r + mid, TILE * (r + 1), k_bf[0])
         for u in range(H):
             scores(u)
         pack_q(q_rest, TILE, NQ)
         quantize(q_mx, TILE, 2 * TILE, q_bf)
         quantize(q_mx, 2 * TILE, NQ, q_bf)
-        pack_k(k1_raw, 1, 0, P)
+        pack_k(nc.vector.tensor_copy, k1_raw, 0, 1, 0, P)
 
         extras = [
             lambda: quantize(k_mx[1], 0, K_PASS, k_bf[1]),
@@ -194,22 +213,45 @@ def tile_rows_cap_kernel(tc, qT, kT, t, v, out):
             lambda: pack_v(1),
             lambda: quantize(v_mx[1], 0, H * D, v_bf[1]),
         ]
+        last = len(SPANS) - 1
         cap(0)
+        scores(H)
         next_unit = 1
-        for n, span in enumerate(SPANS):
-            while next_unit <= min(span[-1] + 1, len(UNITS) - 1):
+        for n, span in enumerate(SPANS[:last - 1]):
+            width = len(span) * TILE
+            while next_unit <= span[-1] + 1:
                 cap(next_unit)
+                if next_unit + H < len(UNITS):
+                    scores(next_unit + H)
                 next_unit = next_unit + 1
-            exponentiate(n)
+            exponentiate(n, 0, width)
             done = values(n - 1) if n > 0 else None
-            weigh(n)
+            weigh(n, 0, width)
             if n < len(extras):
                 extras[n]()
             if done is not None:
                 invert(done)
-            quantize_weights(n)
+            quantize_weights(n, 0, width)
             if done is not None:
                 normalize(done)
-        done = values(len(SPANS) - 1)
-        invert(done)
-        normalize(done)
+
+        mid = TILE // 2
+        final = SPANS[last][0]
+        cap(final, 0, mid)
+        exponentiate(last - 1, 0, TILE)
+        cap(final, mid, TILE)
+        exponentiate(last, 0, mid)
+        exponentiate(last, mid, TILE)
+        third_last = values(last - 2)
+        weigh(last - 1, 0, TILE)
+        weigh(last, 0, mid)
+        weigh(last, mid, TILE)
+        quantize_weights(last - 1, 0, TILE)
+        quantize_weights(last, 0, mid)
+        quantize_weights(last, mid, TILE)
+        invert(third_last)
+        normalize_on_scalar(third_last)
+        for n in (last - 1, last):
+            done = values(n)
+            invert(done)
+            normalize_on_scalar(done)

@@ -26,7 +26,10 @@ SCALAR_SHARE = 20
 GROUPS = [(0, 0), (0, 1), (1, 0), (1, 1), (0, 2), (1, 2), (0, 3), (1, 3)]
 UNITS = [(g, c, h) for g, c in GROUPS for h in range(H)]
 LAST_GROUP = len(UNITS) - H
-SPANS = [(u, u + 1) for u in range(0, LAST_GROUP, 2)] + [(u,) for u in range(LAST_GROUP, len(UNITS))]
+PAIRS_FROM = LAST_GROUP - 2 * H
+SPANS = ([tuple(range(u, u + H)) for u in range(0, PAIRS_FROM, H)]
+         + [(u, u + 1) for u in range(PAIRS_FROM, LAST_GROUP, 2)]
+         + [(u,) for u in range(LAST_GROUP, len(UNITS))])
 
 
 def tile_rows_cap_kernel(tc, qT, kT, t, v, out):
@@ -112,13 +115,13 @@ def tile_rows_cap_kernel(tc, qT, kT, t, v, out):
 
         def cap(u, first=0, last=TILE):
             n, i = span_of[u]
-            dst = words(span_tile(capped, n, "capped", F32, 4), i * TILE + first, i * TILE + last)
+            dst = words(span_tile(capped, n, "capped", F32, 3), i * TILE + first, i * TILE + last)
             src = score_banks[UNITS[u][2]][:].rearrange("p (r q) -> p q r", r=PACK)[:, first:last]
             nc.scalar.activation(out=dst, in_=src, func=ACT.Tanh, scale=1.0 / CAP)
 
         def exponentiate(n, first, last):
             cols = slice(PACK * first, PACK * last)
-            nc.scalar.activation(out=span_tile(probs, n, "probs", F32, 8)[:, cols], in_=capped[n][:, cols],
+            nc.scalar.activation(out=span_tile(probs, n, "probs", F32, 5)[:, cols], in_=capped[n][:, cols],
                                  func=ACT.Exp, scale=CAP)
 
         def weigh(n, first, last):
@@ -206,18 +209,18 @@ def tile_rows_cap_kernel(tc, qT, kT, t, v, out):
         quantize(q_mx, 2 * TILE, NQ, q_bf)
         pack_k(nc.vector.tensor_copy, k1_raw, 0, 1, 0, P)
 
+        quantize(k_mx[1], 0, K_PASS, k_bf[1])
+        pack_v(0)
+
         extras = [
-            lambda: quantize(k_mx[1], 0, K_PASS, k_bf[1]),
-            lambda: pack_v(0),
-            lambda: quantize(v_mx[0], 0, H * D, v_bf[0]),
-            lambda: pack_v(1),
-            lambda: quantize(v_mx[1], 0, H * D, v_bf[1]),
+            [lambda: quantize(v_mx[0], 0, H * D, v_bf[0]), lambda: pack_v(1)],
+            [lambda: quantize(v_mx[1], 0, H * D, v_bf[1])],
         ]
-        last = len(SPANS) - 1
+        first_single = len(SPANS) - H
         cap(0)
         scores(H)
         next_unit = 1
-        for n, span in enumerate(SPANS[:last - 1]):
+        for n, span in enumerate(SPANS[:first_single]):
             width = len(span) * TILE
             while next_unit <= span[-1] + 1:
                 cap(next_unit)
@@ -227,31 +230,32 @@ def tile_rows_cap_kernel(tc, qT, kT, t, v, out):
             exponentiate(n, 0, width)
             done = values(n - 1) if n > 0 else None
             weigh(n, 0, width)
-            if n < len(extras):
-                extras[n]()
+            for extra in extras[n] if n < len(extras) else []:
+                extra()
             if done is not None:
                 invert(done)
-            quantize_weights(n, 0, width)
+            if n + 1 < first_single:
+                quantize_weights(n, 0, width)
             if done is not None:
                 normalize(done)
 
+        last = len(SPANS) - 1
         mid = TILE // 2
-        final = SPANS[last][0]
-        cap(final, 0, mid)
-        exponentiate(last - 1, 0, TILE)
-        cap(final, mid, TILE)
-        exponentiate(last, 0, mid)
-        exponentiate(last, mid, TILE)
-        third_last = values(last - 2)
-        weigh(last - 1, 0, TILE)
-        weigh(last, 0, mid)
-        weigh(last, mid, TILE)
+        for n in range(first_single, last):
+            following = SPANS[n + 1][0]
+            cap(following, 0, TILE if n + 1 < last else mid)
+            exponentiate(n, 0, TILE)
+            weigh(n, 0, TILE)
+            quantize_weights(n - 1, 0, len(SPANS[n - 1]) * TILE)
+        cap(SPANS[last][0], mid, TILE)
+        for first in (0, mid):
+            exponentiate(last, first, first + mid)
+            weigh(last, first, first + mid)
         quantize_weights(last - 1, 0, TILE)
-        quantize_weights(last, 0, mid)
-        quantize_weights(last, mid, TILE)
-        invert(third_last)
-        normalize_on_scalar(third_last)
-        for n in (last - 1, last):
+        for first in (0, mid):
+            quantize_weights(last, first, first + mid)
+        values(first_single - 1)
+        for n in range(first_single, last + 1):
             done = values(n)
             invert(done)
             normalize_on_scalar(done)

@@ -26,9 +26,10 @@ SCALAR_SHARE = 20
 GROUPS = [(0, 0), (0, 1), (1, 0), (1, 1), (0, 2), (1, 2), (0, 3), (1, 3)]
 UNITS = [(g, c, h) for g, c in GROUPS for h in range(H)]
 LAST_GROUP = len(UNITS) - H
-PAIRS_FROM = LAST_GROUP - 2 * H
-SPANS = ([tuple(range(u, u + H)) for u in range(0, PAIRS_FROM, H)]
-         + [(u, u + 1) for u in range(PAIRS_FROM, LAST_GROUP, 2)]
+WIDE_FROM, WIDE_TO = 2 * H, 4 * H
+SPANS = ([(u, u + 1) for u in range(0, WIDE_FROM, 2)]
+         + [tuple(range(u, u + H)) for u in range(WIDE_FROM, WIDE_TO, H)]
+         + [(u, u + 1) for u in range(WIDE_TO, LAST_GROUP, 2)]
          + [(u,) for u in range(LAST_GROUP, len(UNITS))])
 
 
@@ -76,9 +77,10 @@ def tile_rows_cap_kernel(tc, qT, kT, t, v, out):
         k_mx = [mx_tiles("k%d" % g, K_PASS) for g in range(PASSES)]
         v_mx = [mx_tiles("v%d" % g, H * D) for g in range(PASSES)]
 
-        def pack_q(raw, first, last):
+        def pack_q(raw, raw_first, first, last):
             dst = q_bf[:, PACK * first:PACK * last].rearrange("p (c i j) -> p c j i", i=4, j=PACK)
-            nc.vector.tensor_copy(out=dst, in_=raw[:].rearrange("p j (c i) -> p c j i", i=4))
+            src = raw[:, :, first - raw_first:last - raw_first].rearrange("p j (c i) -> p c j i", i=4)
+            nc.vector.tensor_copy(out=dst, in_=src)
 
         def pack_k(copy, raw, raw_first, g, first, last):
             dst = k_bf[g][:].rearrange("p (r s j) -> p s r j", r=PACK, j=PACK)[:, first:last]
@@ -121,7 +123,7 @@ def tile_rows_cap_kernel(tc, qT, kT, t, v, out):
 
         def exponentiate(n, first, last):
             cols = slice(PACK * first, PACK * last)
-            nc.scalar.activation(out=span_tile(probs, n, "probs", F32, 5)[:, cols], in_=capped[n][:, cols],
+            nc.scalar.activation(out=span_tile(probs, n, "probs", F32, 6)[:, cols], in_=capped[n][:, cols],
                                  func=ACT.Exp, scale=CAP)
 
         def weigh(n, first, last):
@@ -192,7 +194,7 @@ def tile_rows_cap_kernel(tc, qT, kT, t, v, out):
             dst = out[h0:h0 + heads, TILE * c:TILE * (c + 1), :].rearrange("h q e -> q h e")
             nc.sync.dma_start(out=dst, in_=res[:])
 
-        pack_q(q_first, 0, TILE)
+        pack_q(q_first, 0, 0, TILE)
         mid = P // 2
         pack_k(nc.vector.tensor_copy, k0_halves[0], 0, 0, 0, mid)
         quantize(q_mx, 0, TILE, q_bf)
@@ -204,17 +206,19 @@ def tile_rows_cap_kernel(tc, qT, kT, t, v, out):
             quantize(k_mx[0], TILE * r + mid, TILE * (r + 1), k_bf[0])
         for u in range(H):
             scores(u)
-        pack_q(q_rest, TILE, NQ)
+        pack_q(q_rest, TILE, TILE, 2 * TILE)
+        pack_q(q_rest, TILE, 2 * TILE, NQ)
         quantize(q_mx, TILE, 2 * TILE, q_bf)
         quantize(q_mx, 2 * TILE, NQ, q_bf)
         pack_k(nc.vector.tensor_copy, k1_raw, 0, 1, 0, P)
 
-        quantize(k_mx[1], 0, K_PASS, k_bf[1])
-        pack_v(0)
 
         extras = [
-            [lambda: quantize(v_mx[0], 0, H * D, v_bf[0]), lambda: pack_v(1)],
-            [lambda: quantize(v_mx[1], 0, H * D, v_bf[1])],
+            lambda: quantize(k_mx[1], 0, K_PASS, k_bf[1]),
+            lambda: pack_v(0),
+            lambda: quantize(v_mx[0], 0, H * D, v_bf[0]),
+            lambda: pack_v(1),
+            lambda: quantize(v_mx[1], 0, H * D, v_bf[1]),
         ]
         first_single = len(SPANS) - H
         cap(0)
@@ -230,8 +234,8 @@ def tile_rows_cap_kernel(tc, qT, kT, t, v, out):
             exponentiate(n, 0, width)
             done = values(n - 1) if n > 0 else None
             weigh(n, 0, width)
-            for extra in extras[n] if n < len(extras) else []:
-                extra()
+            if n < len(extras):
+                extras[n]()
             if done is not None:
                 invert(done)
             if n + 1 < first_single:

from contextlib import ExitStack

import concourse.mybir as mybir

H, D, NQ, N = 4, 128, 512, 1024
CAP = 2.0
FLOPS = 2 * 2 * H * NQ * N * D

F32 = mybir.dt.float32
BF16 = mybir.dt.bfloat16
U32 = mybir.dt.uint32
U8 = mybir.dt.uint8
FP8X4 = mybir.dt.float8_e4m3fn_x4
ACT = mybir.ActivationFunctionType
ALU = mybir.AluOpType

P = 128
PACK = 4
ROWS = D // PACK
K_PASS = P * PACK
TILE = 128
CHUNKS = NQ // TILE
PASSES = N // K_PASS

SCALAR_SHARE = 20
GROUPS = [(0, 0), (0, 1), (1, 0), (1, 1), (0, 2), (1, 2), (0, 3), (1, 3)]
UNITS = [(g, c, h) for g, c in GROUPS for h in range(H)]
LAST_GROUP = len(UNITS) - H
WIDE_FROM, WIDE_TO = 2 * H, 4 * H
SPANS = ([(u, u + 1) for u in range(0, WIDE_FROM, 2)]
         + [tuple(range(u, u + H)) for u in range(WIDE_FROM, WIDE_TO, H)]
         + [(u, u + 1) for u in range(WIDE_TO, LAST_GROUP, 2)]
         + [(u,) for u in range(LAST_GROUP, len(UNITS))])


def tile_rows_cap_kernel(tc, qT, kT, t, v, out):
    nc = tc.nc
    q_rows = qT.rearrange("h d q -> (h d) q").rearrange("(p j) q -> p j q", j=PACK)
    k_rows = kT.rearrange("h d n -> (h d) n").rearrange("(p j) n -> p j n", j=PACK)

    with ExitStack() as ctx:
        keep = ctx.enter_context(tc.tile_pool(name="keep", bufs=1))
        work = ctx.enter_context(tc.tile_pool(name="work", bufs=1))
        score_pool = ctx.enter_context(tc.psum_pool(name="scores", bufs=1))
        y_pool = ctx.enter_context(tc.psum_pool(name="y", bufs=4))
        ctx.enter_context(tc.manual_schedule())

        def load(name, src):
            raw = keep.tile([P] + list(src.shape[1:]), F32, name=name, align_bytes=64)
            nc.sync.dma_start(out=raw[:], in_=src)
            return raw

        def mx_tiles(name, words):
            codes = keep.tile([P, words], U32, name=name + "_codes", align_bytes=64)
            scales = keep.tile([P, words], U8, name=name + "_scales", align_bytes=64)
            return codes, scales

        def quantize(mx, first, last, packed):
            codes, scales = mx
            nc.vector.quantize_mx(out=codes[:, first:last].bitcast(FP8X4), scales=scales[:, first:last],
                                  in_=packed[:, PACK * first:PACK * last])

        half = K_PASS // 2
        q_first = load("q_first", q_rows[:, :, 0:TILE])
        k0_halves = [load("k0_%d" % i, k_rows[:, :, i * half:(i + 1) * half]) for i in range(2)]
        t_tile = keep.tile([P, PASSES, 8], F32, name="t_tile", align_bytes=64)
        nc.sync.dma_start(out=t_tile[:, :, 0:PACK], in_=t.rearrange("(g p j) o -> p g (j o)", g=PASSES, j=PACK))
        q_rest = load("q_rest", q_rows[:, :, TILE:NQ])
        k1_raw = load("k1", k_rows[:, :, K_PASS:N])
        v_raw = [load("v%d" % g, v[:, g * K_PASS:(g + 1) * K_PASS, :].rearrange("h (p j) e -> p h (j e)", j=PACK))
                 for g in range(PASSES)]

        q_bf = keep.tile([P, NQ * PACK], BF16, name="q_bf", align_bytes=64)
        k_bf = [keep.tile([P, K_PASS * PACK], BF16, name="k_bf%d" % g, align_bytes=64) for g in range(PASSES)]
        v_bf = [keep.tile([P, H * D * PACK], BF16, name="v_bf%d" % g, align_bytes=64) for g in range(PASSES)]
        q_mx = mx_tiles("q", NQ)
        k_mx = [mx_tiles("k%d" % g, K_PASS) for g in range(PASSES)]
        v_mx = [mx_tiles("v%d" % g, H * D) for g in range(PASSES)]

        def pack_q(raw, raw_first, first, last):
            dst = q_bf[:, PACK * first:PACK * last].rearrange("p (c i j) -> p c j i", i=4, j=PACK)
            src = raw[:, :, first - raw_first:last - raw_first].rearrange("p j (c i) -> p c j i", i=4)
            nc.vector.tensor_copy(out=dst, in_=src)

        def pack_k(copy, raw, raw_first, g, first, last):
            dst = k_bf[g][:].rearrange("p (r s j) -> p s r j", r=PACK, j=PACK)[:, first:last]
            src = raw[:].rearrange("p j (s r) -> p s r j", r=PACK)[:, first - raw_first:last - raw_first]
            copy(out=dst, in_=src)

        def pack_v(g):
            dst = v_bf[g][:].rearrange("p (h c i j) -> p h c j i", h=H, i=4, j=PACK)
            nc.vector.tensor_copy(out=dst, in_=v_raw[g][:].rearrange("p h (j c i) -> p h c j i", j=PACK, i=4))

        score_banks = [score_pool.tile([P, PACK * TILE], F32, name="scores%d" % h) for h in range(H)]

        def scores(u):
            g, c, h = UNITS[u]
            rows = slice(ROWS * h, ROWS * (h + 1))
            cols = slice(TILE * c, TILE * (c + 1))
            for r in range(PACK):
                place = slice(TILE * r, TILE * (r + 1))
                nc.tensor.matmul_mx(out=score_banks[h][:, place],
                                    lhsT=k_mx[g][0][rows, place].bitcast(FP8X4), lhsT_scale=k_mx[g][1][rows, place],
                                    rhs=q_mx[0][rows, cols].bitcast(FP8X4), rhs_scale=q_mx[1][rows, cols],
                                    start=True, stop=True)

        capped, probs, weights, w_mx, y_tiles, recips = {}, {}, {}, {}, {}, {}
        span_of = {u: (n, i) for n, span in enumerate(SPANS) for i, u in enumerate(span)}

        def span_tile(table, n, name, dtype, bufs):
            if n not in table:
                table[n] = work.tile([P, len(SPANS[n]) * K_PASS], dtype, name=name, bufs=bufs, align_bytes=64)
            return table[n]

        def words(tile, first, last):
            return tile[:, PACK * first:PACK * last].rearrange("p (q r) -> p q r", r=PACK)

        def cap(u, first=0, last=TILE):
            n, i = span_of[u]
            dst = words(span_tile(capped, n, "capped", F32, 3), i * TILE + first, i * TILE + last)
            src = score_banks[UNITS[u][2]][:].rearrange("p (r q) -> p q r", r=PACK)[:, first:last]
            nc.scalar.activation(out=dst, in_=src, func=ACT.Tanh, scale=1.0 / CAP)

        def exponentiate(n, first, last):
            cols = slice(PACK * first, PACK * last)
            nc.scalar.activation(out=span_tile(probs, n, "probs", F32, 6)[:, cols], in_=capped[n][:, cols],
                                 func=ACT.Exp, scale=CAP)

        def weigh(n, first, last):
            g = UNITS[SPANS[n][0]][0]
            nc.vector.tensor_tensor(out=words(span_tile(weights, n, "weights", BF16, 4), first, last),
                                    in0=words(probs[n], first, last),
                                    in1=t_tile[:, g, 0:PACK].unsqueeze(1).to_broadcast([P, last - first, PACK]),
                                    op=ALU.mult)

        def quantize_weights(n, first, last):
            if n not in w_mx:
                w_mx[n] = mx_tiles("w%d" % n, len(SPANS[n]) * TILE)
            quantize(w_mx[n], first, last, weights[n])

        def y_slot(c, h):
            key = (c, h) if c == CHUNKS - 1 else (c, 0)
            heads = 1 if c == CHUNKS - 1 else H
            if key not in y_tiles:
                y_tiles[key] = y_pool.tile([P, heads, D], F32, name="y")
            return y_tiles[key][:, h - key[1], :]

        def value_pass(g, c, h):
            n, i = span_of[UNITS.index((g, c, h))]
            place = slice(TILE * i, TILE * (i + 1))
            cols = slice(D * h, D * (h + 1))
            nc.tensor.matmul_mx(out=y_slot(c, h),
                                lhsT=w_mx[n][0][:, place].bitcast(FP8X4), lhsT_scale=w_mx[n][1][:, place],
                                rhs=v_mx[g][0][:, cols].bitcast(FP8X4), rhs_scale=v_mx[g][1][:, cols],
                                start=(g == 0), stop=(g == PASSES - 1))

        def values(n):
            done = None
            for u in SPANS[n]:
                g, c, h = UNITS[u]
                if c == CHUNKS - 1:
                    value_pass(g, c, h)
                    if g == PASSES - 1:
                        done = (c, h)
                elif g == PASSES - 1:
                    for each in range(PASSES):
                        value_pass(each, c, h)
                    if h == H - 1:
                        done = (c, 0)
            return done

        def invert(key):
            y = y_tiles[key]
            heads = y.shape[1]
            recips[key] = work.tile([P, heads, 1], F32, name="recip", bufs=4, align_bytes=64)
            nc.vector.reciprocal(out=recips[key][:], in_=y[:, :, D - 1:D])

        def normalize(key):
            c, h0 = key
            y = y_tiles[key]
            heads = y.shape[1]
            res = work.tile([P, heads, D], F32, name="res", bufs=4, align_bytes=64)
            nc.vector.tensor_tensor(out=res[:], in0=y[:], in1=recips[key][:].to_broadcast([P, heads, D]), op=ALU.mult)
            store(key, res)

        def normalize_on_scalar(key):
            res = work.tile([P, 1, D], F32, name="res", bufs=4, align_bytes=64)
            nc.scalar.activation(out=res[:, 0, :], in_=y_tiles[key][:, 0, :], func=ACT.Copy, scale=recips[key][:, 0, :])
            store(key, res)

        def store(key, res):
            c, h0 = key
            heads = res.shape[1]
            dst = out[h0:h0 + heads, TILE * c:TILE * (c + 1), :].rearrange("h q e -> q h e")
            nc.sync.dma_start(out=dst, in_=res[:])

        pack_q(q_first, 0, 0, TILE)
        mid = P // 2
        pack_k(nc.vector.tensor_copy, k0_halves[0], 0, 0, 0, mid)
        quantize(q_mx, 0, TILE, q_bf)
        for r in range(PACK):
            quantize(k_mx[0], TILE * r, TILE * r + mid, k_bf[0])
        pack_k(nc.vector.tensor_copy, k0_halves[1], mid, 0, mid, P - SCALAR_SHARE)
        pack_k(nc.scalar.copy, k0_halves[1], mid, 0, P - SCALAR_SHARE, P)
        for r in range(PACK):
            quantize(k_mx[0], TILE * r + mid, TILE * (r + 1), k_bf[0])
        for u in range(H):
            scores(u)
        pack_q(q_rest, TILE, TILE, 2 * TILE)
        pack_q(q_rest, TILE, 2 * TILE, NQ)
        quantize(q_mx, TILE, 2 * TILE, q_bf)
        quantize(q_mx, 2 * TILE, NQ, q_bf)
        pack_k(nc.vector.tensor_copy, k1_raw, 0, 1, 0, P)


        extras = [
            lambda: quantize(k_mx[1], 0, K_PASS, k_bf[1]),
            lambda: pack_v(0),
            lambda: quantize(v_mx[0], 0, H * D, v_bf[0]),
            lambda: pack_v(1),
            lambda: quantize(v_mx[1], 0, H * D, v_bf[1]),
        ]
        first_single = len(SPANS) - H
        cap(0)
        scores(H)
        next_unit = 1
        for n, span in enumerate(SPANS[:first_single]):
            width = len(span) * TILE
            while next_unit <= span[-1] + 1:
                cap(next_unit)
                if next_unit + H < len(UNITS):
                    scores(next_unit + H)
                next_unit = next_unit + 1
            exponentiate(n, 0, width)
            done = values(n - 1) if n > 0 else None
            weigh(n, 0, width)
            if n < len(extras):
                extras[n]()
            if done is not None:
                invert(done)
            if n + 1 < first_single:
                quantize_weights(n, 0, width)
            if done is not None:
                normalize(done)

        last = len(SPANS) - 1
        mid = TILE // 2
        for n in range(first_single, last):
            following = SPANS[n + 1][0]
            cap(following, 0, TILE if n + 1 < last else mid)
            exponentiate(n, 0, TILE)
            weigh(n, 0, TILE)
            quantize_weights(n - 1, 0, len(SPANS[n - 1]) * TILE)
        cap(SPANS[last][0], mid, TILE)
        for first in (0, mid):
            exponentiate(last, first, first + mid)
            weigh(last, first, first + mid)
        quantize_weights(last - 1, 0, TILE)
        for first in (0, mid):
            quantize_weights(last, first, first + mid)
        values(first_single - 1)
        for n in range(first_single, last + 1):
            done = values(n)
            invert(done)
            normalize_on_scalar(done)
